import numpy as np
import ml_dtypes


def mxq(x, axis, fmt="e4m3"):
    dtype, down = {"e4m3": (ml_dtypes.float8_e4m3fn, 7), "e5m2": (ml_dtypes.float8_e5m2, 14)}[fmt]
    v = np.moveaxis(np.asarray(x, np.float32).astype(ml_dtypes.bfloat16).astype(np.float64), axis, -1)
    blocks = v.reshape(v.shape[:-1] + (-1, 32))
    amax = np.abs(blocks).max(-1, keepdims=True)
    byte = np.maximum(np.where(amax > 0, np.frexp(amax)[1] - 1 + 127, 0) - down, 1)
    scale = np.exp2(byte - 127.0)
    codes = (blocks / scale).astype(np.float32).astype(dtype).astype(np.float64)
    return np.moveaxis((codes * scale).reshape(v.shape), -1, axis)


WIDE = False


def mx_kscale(k):
    if not WIDE:
        return np.ones(k)
    levels = np.array([10, -10, 5, -5, 0])
    if k % 512:
        return np.exp2(np.random.permutation(np.resize(levels, k // 32))).repeat(32)
    a = np.empty((k // 512, 16))
    for p in range(k // 512):
        a[p, :8] = np.random.permutation(np.resize(levels, 8))
        for g in range(8):
            far = levels[np.abs(levels - a[p, g]) >= 10]
            a[p, g + 8] = far[np.random.randint(len(far))]
    return np.exp2(a.ravel()).repeat(32)


def f64(x):
    return np.asarray(x).astype(np.float64)


def striped(idx):
    return np.tile(idx.reshape(-1, 16).T, (8, 1)).astype(np.uint16)


def unstriped(offs):
    return offs[:16].T.reshape(-1).astype(np.int64)


def striped8(idx):
    return np.concatenate([x.reshape(-1, 16).T for x in idx]).astype(np.uint16)


def runs(offs, k):
    lists = np.stack([offs[16 * r : 16 * r + 16].T.reshape(-1) for r in range(8)]).astype(np.int64)
    return lists[np.arange(k) % 512 // 64]


def pack_weight(w):
    k, n = w.shape
    w = f64(np.asarray(w, np.float32).astype(ml_dtypes.bfloat16)).reshape(k // 32, 32, n)
    amax = np.abs(w).max(1)
    byte = np.clip(np.where(amax > 0, np.frexp(amax)[1] - 1 + 127 - 7, 1), 1, 254)
    scaled = (w * np.exp2(127.0 - byte)[:, None, :]).reshape(k, n).astype(np.float32)
    words = np.ascontiguousarray(scaled.reshape(k // 512, 128, 4, n).transpose(0, 1, 3, 2)).astype(ml_dtypes.float8_e4m3fn).view(np.uint8)
    return words, np.ascontiguousarray(byte.astype(np.uint8).reshape(k // 512, 16, n))


def unpack_weight(words, scales):
    g, p, n, _ = words.shape
    vals = np.ascontiguousarray(words).view(ml_dtypes.float8_e4m3fn).astype(np.float64) * np.repeat(np.exp2(scales.astype(np.float64) - 127.0), 8, axis=1)[..., None]
    return vals.transpose(0, 1, 3, 2).reshape(g * 512, n)

def planes(y):
    n, m = y.shape
    v = y.astype(np.float32).astype(ml_dtypes.bfloat16).astype(np.float64).reshape(n // 32, 32, m)
    top = np.abs(v).max(1)
    byte = np.clip(np.where(top > 0, np.frexp(top)[1] - 1 + 127 - 7, 1), 1, 254)
    codes = (v * np.exp2(127.0 - byte)[:, None, :]).reshape(n, m).astype(np.float32).astype(ml_dtypes.float8_e4m3fn).view(np.uint8)
    words = codes.reshape(n // 512, 128, 4, m).transpose(0, 1, 3, 2)
    return np.ascontiguousarray(words), np.ascontiguousarray(byte.astype(np.uint8).reshape(n // 512, 16, m))


K, T, S, V, H, G, U = 512, 2048, 1024, 512, 512, 2048, 1024


def setup_inputs():
    n = np.random.standard_normal
    s = mx_kscale(K)[:, None]
    packed_xT = pack_weight(n((K, T)) * s)
    packed_w1 = pack_weight(n((K, H)) / np.sqrt(K) / s)
    packed_dT = pack_weight(n((K, G)) / s)
    return {
        "x_words": packed_xT[0],
        "x_scales": packed_xT[1],
        "w1_words": packed_w1[0],
        "w1_scales": packed_w1[1],
        "gs": (np.random.uniform(0.5, 1.5, (K, 1)) * s).astype(np.float32),
        "d_words": packed_dT[0],
        "d_scales": packed_dT[1],
        "mem": n((H, U)).astype(np.float32),
        "offs": striped(np.random.permutation(T)[:S]),
        "n1": striped8(np.stack([np.random.permutation(S) for _ in range(8)])),
        "k1": striped8(np.random.randint(0, G, (8, H))),
        "n2": striped8(np.stack([np.random.permutation(U)[:V] for _ in range(8)])),
    }


def reference(x_words, x_scales, w1_words, w1_scales, gs, d_words, d_scales, mem, offs, n1, k1, n2):
    d_k1 = unpack_weight(d_words, d_scales)[np.arange(K)[:, None], runs(k1, K)]
    xq = unpack_weight(x_words, x_scales)[:, unstriped(offs)]
    y = unpack_weight(w1_words, w1_scales).T @ xq
    ln = y[np.arange(H)[:, None], runs(n1, H)]
    z = f64(gs) * (ln.reshape(H, V, 2).max(axis=2))
    h = 0.0625 * ((d_k1.T @ mxq(z, 0, "e4m3")))
    nw = np.maximum(h, 0.5 * (f64(mem)[np.arange(H)[:, None], runs(n2, H)]))
    out = f64(mem).copy()
    out[np.arange(H)[:, None], runs(n2, H)] = nw
    return (out,) + planes(out)

@@ -1,0 +1,177 @@
+from contextlib import ExitStack
+
+import concourse.mybir as mybir
+
+K, T, S, V, H, G, U = 512, 2048, 1024, 512, 512, 2048, 1024
+FLOPS = 2 * K * H * S + 2 * K * H * V
+
+F32 = mybir.dt.float32
+BF16 = mybir.dt.bfloat16
+I32 = mybir.dt.int32
+U32 = mybir.dt.uint32
+U16 = mybir.dt.uint16
+U8 = mybir.dt.uint8
+FP8X4 = mybir.dt.float8_e4m3fn_x4
+ALU = mybir.AluOpType
+COPY = mybir.ActivationFunctionType.Copy
+
+P = 128
+PACK = 4
+LIST_ROWS = 16
+
+
+def tile_picked_densepoolpagex_none_po_kernel(
+    tc, x_words, x_scales, w1_words, w1_scales, gs, d_words, d_scales, mem, offs, n1, k1, n2, out_0, out_1, out_2
+):
+    nc = tc.nc
+    with ExitStack() as ctx:
+        sb = ctx.enter_context(tc.tile_pool(name="sb", bufs=1))
+        ps = ctx.enter_context(tc.psum_pool(name="ps", bufs=1))
+
+        def tile(shape, dtype, name, tag=None):
+            return sb.tile(shape, dtype, name=name, tag=tag or name, align_bytes=64)
+
+        def words_view(dram):
+            return dram[0].rearrange("p n t -> p (n t)").bitcast(I32)
+
+        offs_t = sb.tile([P, S // LIST_ROWS], U16, name="offs_t")
+        n1_t = sb.tile([P, S // LIST_ROWS], U16, name="n1_t")
+        k1_t = sb.tile([P, H // LIST_ROWS], U16, name="k1_t")
+        n2_t = sb.tile([P, V // LIST_ROWS], U16, name="n2_t")
+
+        xs_win = tile([P, T], U8, "xs_win")
+        ds_win = tile([P, G], U8, "ds_win")
+        ws_raw = tile([P, H], U8, "ws_raw")
+        ds_fin = tile([P, H], U8, "ds_fin")
+        xw_win = tile([P, T], I32, "xw_win")
+        dw_win = tile([P, G], I32, "dw_win")
+        ww_raw = tile([P, H], I32, "ww_raw")
+        gs_t = tile([P, PACK], F32, "gs_t")
+        page = [tile([P, U], F32, "page%d" % t) for t in range(PACK)]
+
+        nc.vector.memset(xs_win[:].bitcast(I32), 0)
+        nc.vector.memset(ws_raw[:].bitcast(I32), 0)
+        nc.vector.memset(ds_win[:].bitcast(I32), 0)
+        nc.vector.memset(ds_fin[:].bitcast(I32), 0)
+
+        nc.sync.dma_start(offs_t[:], offs)
+        for q in range(4):
+            nc.sync.dma_start(xs_win[32 * q : 32 * q + 4, :].bitcast(I32), x_scales[0, 4 * q : 4 * q + 4, :].bitcast(I32))
+        nc.sync.dma_start(xw_win[:], words_view(x_words))
+        nc.sync.dma_start(ww_raw[:], words_view(w1_words))
+        nc.sync.dma_start(k1_t[:], k1)
+        for q in range(4):
+            nc.sync.dma_start(ws_raw[32 * q : 32 * q + 4, :].bitcast(I32), w1_scales[0, 4 * q : 4 * q + 4, :].bitcast(I32))
+        for j in range(2):
+            nc.sync.dma_start(ds_win[j:P:16, :].bitcast(I32), d_scales[0, j:16:2, :].bitcast(I32))
+        nc.sync.dma_start(dw_win[:], words_view(d_words))
+        nc.sync.dma_start(n1_t[:], n1)
+        nc.sync.dma_start(gs_t[:], gs.rearrange("(p t) o -> p (t o)", t=PACK))
+        nc.sync.dma_start(n2_t[:], n2)
+        mem_rows = mem.rearrange("(p t) c -> p t c", t=PACK)
+        for t in range(PACK):
+            nc.sync.dma_start(page[t][:], mem_rows[:, t, :])
+
+        def deal(dst, src):
+            nc.vector.tensor_copy(dst.rearrange("p (t m) -> p t m", t=PACK), src.rearrange("p (m t) -> p t m", t=PACK))
+
+        xs_g = tile([P, S], U8, "xs_g")
+        nc.vector.tensor_copy(xs_g[:], xs_win[:].indirect(offs_t[:]))
+        ww = tile([P, H], I32, "ww")
+        ws = tile([P, H], U8, "ws")
+        deal(ww[:], ww_raw[:])
+        deal(ws[:], ws_raw[:])
+        xw_g = [tile([P, 512], U32, "xw_g%d" % a) for a in range(2)]
+        for a in range(2):
+            nc.vector.tensor_copy(xw_g[a][:], xw_win[:].bitcast(U32).indirect(offs_t[:, 32 * a : 32 * a + 32]))
+
+        y = [tile([P, S], F32, "y%d" % t) for t in range(PACK)]
+        for t, a in ((0, 0), (1, 0), (0, 1), (1, 1), (2, 0), (2, 1), (3, 0), (3, 1)):
+            acc = ps.tile([P, 512], F32, name="acc", tag="bank%d" % (2 * t + a))
+            nc.tensor.matmul_mx(
+                out=acc[:],
+                lhsT=ww[:, P * t : P * (t + 1)].bitcast(FP8X4),
+                lhsT_scale=ws[:, P * t : P * (t + 1)],
+                rhs=xw_g[a][:].bitcast(FP8X4),
+                rhs_scale=xs_g[:, 512 * a : 512 * (a + 1)],
+                start=True,
+                stop=True,
+            )
+            nc.scalar.copy(y[t][:, 512 * a : 512 * (a + 1)], acc[:])
+
+        ds_g = tile([P, H], U8, "ds_g")
+        dw_g = tile([P, H], U32, "dw_g")
+        nc.vector.tensor_copy(ds_g[:], ds_win[:].indirect(k1_t[:]))
+        nc.vector.tensor_copy(dw_g[:], dw_win[:].bitcast(U32).indirect(k1_t[:]))
+        ds_d = tile([P, H], U8, "ds_d")
+        dw = tile([P, H], I32, "dw")
+        deal(ds_d[:], ds_g[:])
+        deal(dw[:], dw_g[:].bitcast(I32))
+        for r in range(4):
+            src = 16 * (r // 2) + r % 2
+            nc.sync.dma_start(ds_fin[r:P:32, :].bitcast(I32), ds_d[src:P:32, :].bitcast(I32))
+
+        hb = [ps.tile([P, V], F32, name="hb%d" % t, tag="bank%d" % t) for t in range(PACK)]
+        held = [None] * PACK
+        for a in range(2):
+            zb = tile([P, 256, PACK], BF16, "zb%d" % a)
+            for u in range(2):
+                ln = tile([P, 2, 512], F32, "ln%d%d" % (a, u))
+                for j in range(2):
+                    nc.vector.tensor_copy(ln[:, j, :], y[2 * u + j][:].indirect(n1_t[:, 32 * a : 32 * a + 32]))
+                if a == 1 and u == 1:
+                    held[0] = tile([P, V], F32, "held0", tag="y3")
+                    nc.vector.tensor_scalar(held[0][:], page[0][:].indirect(n2_t[:]), 0.5, 0.0, ALU.mult, ALU.add)
+                pairs = ln[:].rearrange("p j (v two) -> p (j v) two", two=2)
+                mx = tile([P, 2, 256], F32, "mx%d%d" % (a, u))
+                nc.vector.tensor_tensor(mx[:].rearrange("p j v -> p (j v)"), pairs[:, :, 0], pairs[:, :, 1], ALU.max)
+                for j in range(2):
+                    t = 2 * u + j
+                    nc.scalar.activation(zb[:, :, t], mx[:, j, :], COPY, scale=gs_t[:, t : t + 1])
+            if a == 1:
+                two = tile([P, 2, V], F32, "held12", tag="ln11")
+                for j in range(2):
+                    held[1 + j] = two[:, j, :]
+                    nc.vector.tensor_scalar(two[:, j, :], page[1 + j][:].indirect(n2_t[:]), 0.5, 0.0, ALU.mult, ALU.add)
+            zw = tile([P, 256], U32, "zw%d" % a)
+            zs = tile([P, 256], U8, "zs%d" % a)
+            nc.vector.quantize_mx(out=zw[:].bitcast(FP8X4), scales=zs[:], in_=zb[:].rearrange("p v t -> p (v t)"))
+            for t in range(PACK):
+                nc.tensor.matmul_mx(
+                    out=hb[t][:, 256 * a : 256 * (a + 1)],
+                    lhsT=dw[:, P * t : P * (t + 1)].bitcast(FP8X4),
+                    lhsT_scale=ds_fin[:, P * t : P * (t + 1)],
+                    rhs=zw[:].bitcast(FP8X4),
+                    rhs_scale=zs[:],
+                    start=True,
+                    stop=True,
+                )
+        held[3] = tile([P, V], F32, "held3", tag="zb1")
+        nc.vector.tensor_scalar(held[3][:], page[3][:].indirect(n2_t[:]), 0.5, 0.0, ALU.mult, ALU.add)
+
+        out_rows = out_0.rearrange("(p t) c -> p t c", t=PACK)
+        ob = [tile([P, 512, PACK], BF16, "ob%d" % c) for c in range(2)]
+        for t in range(PACK):
+            nw = tile([P, V], F32, "nw%d" % t)
+            nc.vector.scalar_tensor_tensor(nw[:], hb[t][:], 0.0625, held[t][:, :], ALU.mult, ALU.max)
+            nc.vector.tensor_copy(page[t][:].indirect(n2_t[:]), nw[:])
+            nc.sync.dma_start(out_rows[:, t, :], page[t][:])
+            if t == 2:
+                nc.scalar.copy(ob[0][:, :, 2:4], page[t][:, 0:512].unsqueeze(2).to_broadcast([P, 512, 2]))
+            elif t == 3:
+                nc.vector.tensor_copy(ob[0][:, :, t], page[t][:, 0:512])
+            else:
+                nc.scalar.copy(ob[0][:, :, t], page[t][:, 0:512])
+            nc.scalar.copy(ob[1][:, :, t], page[t][:, 512:1024])
+
+        osc = tile([P, U], U8, "osc")
+        out_words = words_view(out_1)
+        for c in range(2):
+            ow = tile([P, 512], I32, "ow%d" % c)
+            nc.vector.quantize_mx(
+                out=ow[:].bitcast(FP8X4), scales=osc[:, 512 * c : 512 * (c + 1)], in_=ob[c][:].rearrange("p v t -> p (v t)")
+            )
+            nc.sync.dma_start(out_words[:, 512 * c : 512 * (c + 1)], ow[:])
+        for q in range(4):
+            eng = nc.scalar if q % 2 else nc.sync
+            eng.dma_start(out_2[0, 4 * q : 4 * q + 4, :].bitcast(I32), osc[32 * q : 32 * q + 4, :].bitcast(I32))

@@ -55,11 +55,11 @@ def tile_picked_densepoolpagex_none_po_kernel(
         nc.vector.memset(ds_fin[:].bitcast(I32), 0)
 
         nc.sync.dma_start(offs_t[:], offs)
+        nc.sync.dma_start(ww_raw[:], words_view(w1_words))
+        nc.sync.dma_start(k1_t[:], k1)
         for q in range(4):
             nc.sync.dma_start(xs_win[32 * q : 32 * q + 4, :].bitcast(I32), x_scales[0, 4 * q : 4 * q + 4, :].bitcast(I32))
         nc.sync.dma_start(xw_win[:], words_view(x_words))
-        nc.sync.dma_start(ww_raw[:], words_view(w1_words))
-        nc.sync.dma_start(k1_t[:], k1)
         for q in range(4):
             nc.sync.dma_start(ws_raw[32 * q : 32 * q + 4, :].bitcast(I32), w1_scales[0, 4 * q : 4 * q + 4, :].bitcast(I32))
         for j in range(2):
@@ -73,7 +73,7 @@ def tile_picked_densepoolpagex_none_po_kernel(
             nc.sync.dma_start(page[t][:], mem_rows[:, t, :])
 
         def deal(dst, src):
-            nc.vector.tensor_copy(dst.rearrange("p (t m) -> p t m", t=PACK), src.rearrange("p (m t) -> p t m", t=PACK))
+            nc.vector.tensor_copy(dst.rearrange("p (t m) -> p m t", t=PACK), src.rearrange("p (m t) -> p m t", t=PACK))
 
         xs_g = tile([P, S], U8, "xs_g")
         nc.vector.tensor_copy(xs_g[:], xs_win[:].indirect(offs_t[:]))
@@ -86,7 +86,7 @@ def tile_picked_densepoolpagex_none_po_kernel(
             nc.vector.tensor_copy(xw_g[a][:], xw_win[:].bitcast(U32).indirect(offs_t[:, 32 * a : 32 * a + 32]))
 
         y = [tile([P, S], F32, "y%d" % t) for t in range(PACK)]
-        for t, a in ((0, 0), (1, 0), (0, 1), (1, 1), (2, 0), (2, 1), (3, 0), (3, 1)):
+        for t, a in [(t, a) for t in range(PACK) for a in range(2)]:
             acc = ps.tile([P, 512], F32, name="acc", tag="bank%d" % (2 * t + a))
             nc.tensor.matmul_mx(
                 out=acc[:],
@@ -112,30 +112,31 @@ def tile_picked_densepoolpagex_none_po_kernel(
             nc.sync.dma_start(ds_fin[r:P:32, :].bitcast(I32), ds_d[src:P:32, :].bitcast(I32))
 
         hb = [ps.tile([P, V], F32, name="hb%d" % t, tag="bank%d" % t) for t in range(PACK)]
+        zb = [tile([P, 256, PACK], BF16, "zb%d" % a) for a in range(2)]
+        ln = [tile([P, 2, 512], F32, "ln%d" % s) for s in range(4)]
         held = [None] * PACK
-        for a in range(2):
-            zb = tile([P, 256, PACK], BF16, "zb%d" % a)
-            for u in range(2):
-                ln = tile([P, 2, 512], F32, "ln%d%d" % (a, u))
-                for j in range(2):
-                    nc.vector.tensor_copy(ln[:, j, :], y[2 * u + j][:].indirect(n1_t[:, 32 * a : 32 * a + 32]))
-                if a == 1 and u == 1:
-                    held[0] = tile([P, V], F32, "held0", tag="y3")
-                    nc.vector.tensor_scalar(held[0][:], page[0][:].indirect(n2_t[:]), 0.5, 0.0, ALU.mult, ALU.add)
-                pairs = ln[:].rearrange("p j (v two) -> p (j v) two", two=2)
-                mx = tile([P, 2, 256], F32, "mx%d%d" % (a, u))
-                nc.vector.tensor_tensor(mx[:].rearrange("p j v -> p (j v)"), pairs[:, :, 0], pairs[:, :, 1], ALU.max)
-                for j in range(2):
-                    t = 2 * u + j
-                    nc.scalar.activation(zb[:, :, t], mx[:, j, :], COPY, scale=gs_t[:, t : t + 1])
-            if a == 1:
-                two = tile([P, 2, V], F32, "held12", tag="ln11")
-                for j in range(2):
-                    held[1 + j] = two[:, j, :]
-                    nc.vector.tensor_scalar(two[:, j, :], page[1 + j][:].indirect(n2_t[:]), 0.5, 0.0, ALU.mult, ALU.add)
+
+        def line_up(i):
+            a, t = divmod(i, PACK)
+            nc.vector.tensor_copy(ln[i // 2][:, i % 2, :], y[t][:].indirect(n1_t[:, 32 * a : 32 * a + 32]))
+
+        def pool_pairs(s):
+            a, u = divmod(s, 2)
+            pairs = ln[s][:].rearrange("p j (v two) -> p (j v) two", two=2)
+            mx = tile([P, 2, 256], F32, "mx%d" % s)
+            nc.vector.tensor_tensor(mx[:].rearrange("p j v -> p (j v)"), pairs[:, :, 0], pairs[:, :, 1], ALU.max)
+            for j in range(2):
+                t = 2 * u + j
+                nc.scalar.activation(zb[a][:, :, t], mx[:, j, :], COPY, scale=gs_t[:, t : t + 1])
+
+        def fetch_held(t, dst):
+            held[t] = dst
+            nc.vector.tensor_scalar(dst, page[t][:].indirect(n2_t[:]), 0.5, 0.0, ALU.mult, ALU.add)
+
+        def second_product(a):
             zw = tile([P, 256], U32, "zw%d" % a)
             zs = tile([P, 256], U8, "zs%d" % a)
-            nc.vector.quantize_mx(out=zw[:].bitcast(FP8X4), scales=zs[:], in_=zb[:].rearrange("p v t -> p (v t)"))
+            nc.vector.quantize_mx(out=zw[:].bitcast(FP8X4), scales=zs[:], in_=zb[a][:].rearrange("p v t -> p (v t)"))
             for t in range(PACK):
                 nc.tensor.matmul_mx(
                     out=hb[t][:, 256 * a : 256 * (a + 1)],
@@ -146,15 +147,34 @@ def tile_picked_densepoolpagex_none_po_kernel(
                     start=True,
                     stop=True,
                 )
-        held[3] = tile([P, V], F32, "held3", tag="zb1")
-        nc.vector.tensor_scalar(held[3][:], page[3][:].indirect(n2_t[:]), 0.5, 0.0, ALU.mult, ALU.add)
+
+        for i in range(2 * PACK):
+            line_up(i)
+            if i >= 2 and i % 2 == 0:
+                pool_pairs(i // 2 - 1)
+            if i == 6:
+                second_product(0)
+        fetch_held(0, tile([P, V], F32, "held0", tag="y3")[:])
+        pool_pairs(3)
+        two = tile([P, 2, V], F32, "held12", tag="ln3")
+        fetch_held(1, two[:, 0, :])
+        fetch_held(2, two[:, 1, :])
+        second_product(1)
+        fetch_held(3, tile([P, V], F32, "held3", tag="zb1")[:])
 
         out_rows = out_0.rearrange("(p t) c -> p t c", t=PACK)
-        ob = [tile([P, 512, PACK], BF16, "ob%d" % c) for c in range(2)]
+        spans = ((0, 512), (512, 768), (768, 1024))
+        ob = [tile([P, hi - lo, PACK], BF16, "ob%d" % c) for c, (lo, hi) in enumerate(spans)]
+        nw = [tile([P, V], F32, "nw%d" % t) for t in range(PACK)]
+
+        def larger(t):
+            nc.vector.scalar_tensor_tensor(nw[t][:], hb[t][:], 0.0625, held[t], ALU.mult, ALU.max)
+
+        larger(0)
         for t in range(PACK):
-            nw = tile([P, V], F32, "nw%d" % t)
-            nc.vector.scalar_tensor_tensor(nw[:], hb[t][:], 0.0625, held[t][:, :], ALU.mult, ALU.max)
-            nc.vector.tensor_copy(page[t][:].indirect(n2_t[:]), nw[:])
+            if t + 1 < PACK:
+                larger(t + 1)
+            nc.vector.tensor_copy(page[t][:].indirect(n2_t[:]), nw[t][:])
             nc.sync.dma_start(out_rows[:, t, :], page[t][:])
             if t == 2:
                 nc.scalar.copy(ob[0][:, :, 2:4], page[t][:, 0:512].unsqueeze(2).to_broadcast([P, 512, 2]))
@@ -162,16 +182,16 @@ def tile_picked_densepoolpagex_none_po_kernel(
                 nc.vector.tensor_copy(ob[0][:, :, t], page[t][:, 0:512])
             else:
                 nc.scalar.copy(ob[0][:, :, t], page[t][:, 0:512])
-            nc.scalar.copy(ob[1][:, :, t], page[t][:, 512:1024])
+            for c in (1, 2):
+                nc.scalar.copy(ob[c][:, :, t], page[t][:, spans[c][0] : spans[c][1]])
 
         osc = tile([P, U], U8, "osc")
         out_words = words_view(out_1)
-        for c in range(2):
-            ow = tile([P, 512], I32, "ow%d" % c)
-            nc.vector.quantize_mx(
-                out=ow[:].bitcast(FP8X4), scales=osc[:, 512 * c : 512 * (c + 1)], in_=ob[c][:].rearrange("p v t -> p (v t)")
-            )
-            nc.sync.dma_start(out_words[:, 512 * c : 512 * (c + 1)], ow[:])
+        for c in (1, 0, 2):
+            lo, hi = spans[c]
+            ow = tile([P, hi - lo], I32, "ow%d" % c)
+            nc.vector.quantize_mx(out=ow[:].bitcast(FP8X4), scales=osc[:, lo:hi], in_=ob[c][:].rearrange("p v t -> p (v t)"))
+            nc.sync.dma_start(out_words[:, lo:hi], ow[:])
         for q in range(4):
             eng = nc.scalar if q % 2 else nc.sync
             eng.dma_start(out_2[0, 4 * q : 4 * q + 4, :].bitcast(I32), osc[32 * q : 32 * q + 4, :].bitcast(I32))

@@ -62,9 +62,9 @@ def tile_picked_densepoolpagex_none_po_kernel(
         nc.sync.dma_start(xw_win[:], words_view(x_words))
         for q in range(4):
             nc.sync.dma_start(ws_raw[32 * q : 32 * q + 4, :].bitcast(I32), w1_scales[0, 4 * q : 4 * q + 4, :].bitcast(I32))
+        nc.sync.dma_start(dw_win[:], words_view(d_words))
         for j in range(2):
             nc.sync.dma_start(ds_win[j:P:16, :].bitcast(I32), d_scales[0, j:16:2, :].bitcast(I32))
-        nc.sync.dma_start(dw_win[:], words_view(d_words))
         nc.sync.dma_start(n1_t[:], n1)
         nc.sync.dma_start(gs_t[:], gs.rearrange("(p t) o -> p (t o)", t=PACK))
         nc.sync.dma_start(n2_t[:], n2)
@@ -101,66 +101,65 @@ def tile_picked_densepoolpagex_none_po_kernel(
 
         ds_g = tile([P, H], U8, "ds_g")
         dw_g = tile([P, H], U32, "dw_g")
-        nc.vector.tensor_copy(ds_g[:], ds_win[:].indirect(k1_t[:]))
         nc.vector.tensor_copy(dw_g[:], dw_win[:].bitcast(U32).indirect(k1_t[:]))
+        nc.vector.tensor_copy(ds_g[:], ds_win[:].indirect(k1_t[:]))
         ds_d = tile([P, H], U8, "ds_d")
         dw = tile([P, H], I32, "dw")
-        deal(ds_d[:], ds_g[:])
         deal(dw[:], dw_g[:].bitcast(I32))
+        deal(ds_d[:], ds_g[:])
         for r in range(4):
             src = 16 * (r // 2) + r % 2
             nc.sync.dma_start(ds_fin[r:P:32, :].bitcast(I32), ds_d[src:P:32, :].bitcast(I32))
 
-        hb = [ps.tile([P, V], F32, name="hb%d" % t, tag="bank%d" % t) for t in range(PACK)]
-        zb = [tile([P, 256, PACK], BF16, "zb%d" % a) for a in range(2)]
-        ln = [tile([P, 2, 512], F32, "ln%d" % s) for s in range(4)]
+        zb = tile([P, V, PACK], BF16, "zb")
+        groups = ((0, 3), (3, 5), (5, 7), (7, 8))
+        ln = [tile([P, hi - lo, 512], F32, "ln%d" % s) for s, (lo, hi) in enumerate(groups)]
+        mx = [tile([P, hi - lo, 256], F32, "mx%d" % s) for s, (lo, hi) in enumerate(groups)]
         held = [None] * PACK
 
-        def line_up(i):
-            a, t = divmod(i, PACK)
-            nc.vector.tensor_copy(ln[i // 2][:, i % 2, :], y[t][:].indirect(n1_t[:, 32 * a : 32 * a + 32]))
+        def line_up(s):
+            for i in range(*groups[s]):
+                t, a = divmod(i, 2)
+                nc.vector.tensor_copy(ln[s][:, i - groups[s][0], :], y[t][:].indirect(n1_t[:, 32 * a : 32 * a + 32]))
 
         def pool_pairs(s):
-            a, u = divmod(s, 2)
             pairs = ln[s][:].rearrange("p j (v two) -> p (j v) two", two=2)
-            mx = tile([P, 2, 256], F32, "mx%d" % s)
-            nc.vector.tensor_tensor(mx[:].rearrange("p j v -> p (j v)"), pairs[:, :, 0], pairs[:, :, 1], ALU.max)
-            for j in range(2):
-                t = 2 * u + j
-                nc.scalar.activation(zb[a][:, :, t], mx[:, j, :], COPY, scale=gs_t[:, t : t + 1])
+            nc.vector.tensor_tensor(mx[s][:].rearrange("p j v -> p (j v)"), pairs[:, :, 0], pairs[:, :, 1], ALU.max)
+            for i in range(*groups[s]):
+                t, a = divmod(i, 2)
+                nc.scalar.activation(
+                    zb[:, 256 * a : 256 * (a + 1), t], mx[s][:, i - groups[s][0], :], COPY, scale=gs_t[:, t : t + 1]
+                )
 
         def fetch_held(t, dst):
             held[t] = dst
             nc.vector.tensor_scalar(dst, page[t][:].indirect(n2_t[:]), 0.5, 0.0, ALU.mult, ALU.add)
 
-        def second_product(a):
-            zw = tile([P, 256], U32, "zw%d" % a)
-            zs = tile([P, 256], U8, "zs%d" % a)
-            nc.vector.quantize_mx(out=zw[:].bitcast(FP8X4), scales=zs[:], in_=zb[a][:].rearrange("p v t -> p (v t)"))
-            for t in range(PACK):
-                nc.tensor.matmul_mx(
-                    out=hb[t][:, 256 * a : 256 * (a + 1)],
-                    lhsT=dw[:, P * t : P * (t + 1)].bitcast(FP8X4),
-                    lhsT_scale=ds_fin[:, P * t : P * (t + 1)],
-                    rhs=zw[:].bitcast(FP8X4),
-                    rhs_scale=zs[:],
-                    start=True,
-                    stop=True,
-                )
-
-        for i in range(2 * PACK):
-            line_up(i)
-            if i >= 2 and i % 2 == 0:
-                pool_pairs(i // 2 - 1)
-            if i == 6:
-                second_product(0)
-        fetch_held(0, tile([P, V], F32, "held0", tag="y3")[:])
+        line_up(0)
+        for s in range(1, 4):
+            line_up(s)
+            pool_pairs(s - 1)
+        fetch_held(0, tile([P, V], F32, "held0", tag="y2")[:])
         pool_pairs(3)
-        two = tile([P, 2, V], F32, "held12", tag="ln3")
+        two = tile([P, 2, V], F32, "held12", tag="y3")
         fetch_held(1, two[:, 0, :])
         fetch_held(2, two[:, 1, :])
-        second_product(1)
-        fetch_held(3, tile([P, V], F32, "held3", tag="zb1")[:])
+
+        zw = tile([P, V], U32, "zw")
+        zs = tile([P, V], U8, "zs")
+        nc.vector.quantize_mx(out=zw[:].bitcast(FP8X4), scales=zs[:], in_=zb[:].rearrange("p v t -> p (v t)"))
+        hb = [ps.tile([P, V], F32, name="hb%d" % t, tag="bank%d" % t) for t in range(PACK)]
+        for t in range(PACK):
+            nc.tensor.matmul_mx(
+                out=hb[t][:],
+                lhsT=dw[:, P * t : P * (t + 1)].bitcast(FP8X4),
+                lhsT_scale=ds_fin[:, P * t : P * (t + 1)],
+                rhs=zw[:].bitcast(FP8X4),
+                rhs_scale=zs[:],
+                start=True,
+                stop=True,
+            )
+        fetch_held(3, tile([P, V], F32, "held3", tag="mx3")[:])
 
         out_rows = out_0.rearrange("(p t) c -> p t c", t=PACK)
         spans = ((0, 512), (512, 768), (768, 1024))

from contextlib import ExitStack

import concourse.mybir as mybir

K, T, S, V, H, G, U = 512, 2048, 1024, 512, 512, 2048, 1024
FLOPS = 2 * K * H * S + 2 * K * H * V

F32 = mybir.dt.float32
BF16 = mybir.dt.bfloat16
I32 = mybir.dt.int32
U32 = mybir.dt.uint32
U16 = mybir.dt.uint16
U8 = mybir.dt.uint8
FP8X4 = mybir.dt.float8_e4m3fn_x4
ALU = mybir.AluOpType
COPY = mybir.ActivationFunctionType.Copy

P = 128
PACK = 4
LIST_ROWS = 16


def tile_picked_densepoolpagex_none_po_kernel(
    tc, x_words, x_scales, w1_words, w1_scales, gs, d_words, d_scales, mem, offs, n1, k1, n2, out_0, out_1, out_2
):
    nc = tc.nc
    with ExitStack() as ctx:
        sb = ctx.enter_context(tc.tile_pool(name="sb", bufs=1))
        ps = ctx.enter_context(tc.psum_pool(name="ps", bufs=1))

        def tile(shape, dtype, name, tag=None):
            return sb.tile(shape, dtype, name=name, tag=tag or name, align_bytes=64)

        def words_view(dram):
            return dram[0].rearrange("p n t -> p (n t)").bitcast(I32)

        offs_t = sb.tile([P, S // LIST_ROWS], U16, name="offs_t")
        n1_t = sb.tile([P, S // LIST_ROWS], U16, name="n1_t")
        k1_t = sb.tile([P, H // LIST_ROWS], U16, name="k1_t")
        n2_t = sb.tile([P, V // LIST_ROWS], U16, name="n2_t")

        xs_win = tile([P, T], U8, "xs_win")
        ds_win = tile([P, G], U8, "ds_win")
        ws_raw = tile([P, H], U8, "ws_raw")
        ds_fin = tile([P, H], U8, "ds_fin")
        xw_win = tile([P, T], I32, "xw_win")
        dw_win = tile([P, G], I32, "dw_win")
        ww_raw = tile([P, H], I32, "ww_raw")
        gs_t = tile([P, PACK], F32, "gs_t")
        page = [tile([P, U], F32, "page%d" % t) for t in range(PACK)]

        nc.vector.memset(xs_win[:].bitcast(I32), 0)
        nc.vector.memset(ws_raw[:].bitcast(I32), 0)
        nc.vector.memset(ds_win[:].bitcast(I32), 0)
        nc.vector.memset(ds_fin[:].bitcast(I32), 0)

        nc.sync.dma_start(offs_t[:], offs)
        nc.sync.dma_start(ww_raw[:], words_view(w1_words))
        nc.sync.dma_start(k1_t[:], k1)
        for q in range(4):
            nc.sync.dma_start(xs_win[32 * q : 32 * q + 4, :].bitcast(I32), x_scales[0, 4 * q : 4 * q + 4, :].bitcast(I32))
        nc.sync.dma_start(xw_win[:], words_view(x_words))
        for q in range(4):
            nc.sync.dma_start(ws_raw[32 * q : 32 * q + 4, :].bitcast(I32), w1_scales[0, 4 * q : 4 * q + 4, :].bitcast(I32))
        nc.sync.dma_start(dw_win[:], words_view(d_words))
        for j in range(2):
            nc.sync.dma_start(ds_win[j:P:16, :].bitcast(I32), d_scales[0, j:16:2, :].bitcast(I32))
        nc.sync.dma_start(n1_t[:], n1)
        nc.sync.dma_start(gs_t[:], gs.rearrange("(p t) o -> p (t o)", t=PACK))
        nc.sync.dma_start(n2_t[:], n2)
        mem_rows = mem.rearrange("(p t) c -> p t c", t=PACK)
        for t in range(PACK):
            nc.sync.dma_start(page[t][:], mem_rows[:, t, :])

        def deal(dst, src):
            nc.vector.tensor_copy(dst.rearrange("p (t m) -> p m t", t=PACK), src.rearrange("p (m t) -> p m t", t=PACK))

        xs_g = tile([P, S], U8, "xs_g")
        nc.vector.tensor_copy(xs_g[:], xs_win[:].indirect(offs_t[:]))
        ww = tile([P, H], I32, "ww")
        ws = tile([P, H], U8, "ws")
        deal(ww[:], ww_raw[:])
        deal(ws[:], ws_raw[:])
        xw_g = [tile([P, 512], U32, "xw_g%d" % a) for a in range(2)]
        for a in range(2):
            nc.vector.tensor_copy(xw_g[a][:], xw_win[:].bitcast(U32).indirect(offs_t[:, 32 * a : 32 * a + 32]))

        y = [tile([P, S], F32, "y%d" % t) for t in range(PACK)]
        for t, a in [(t, a) for t in range(PACK) for a in range(2)]:
            acc = ps.tile([P, 512], F32, name="acc", tag="bank%d" % (2 * t + a))
            nc.tensor.matmul_mx(
                out=acc[:],
                lhsT=ww[:, P * t : P * (t + 1)].bitcast(FP8X4),
                lhsT_scale=ws[:, P * t : P * (t + 1)],
                rhs=xw_g[a][:].bitcast(FP8X4),
                rhs_scale=xs_g[:, 512 * a : 512 * (a + 1)],
                start=True,
                stop=True,
            )
            nc.scalar.copy(y[t][:, 512 * a : 512 * (a + 1)], acc[:])

        ds_g = tile([P, H], U8, "ds_g")
        dw_g = tile([P, H], U32, "dw_g")
        nc.vector.tensor_copy(dw_g[:], dw_win[:].bitcast(U32).indirect(k1_t[:]))
        nc.vector.tensor_copy(ds_g[:], ds_win[:].indirect(k1_t[:]))
        ds_d = tile([P, H], U8, "ds_d")
        dw = tile([P, H], I32, "dw")
        deal(dw[:], dw_g[:].bitcast(I32))
        deal(ds_d[:], ds_g[:])
        for r in range(4):
            src = 16 * (r // 2) + r % 2
            nc.sync.dma_start(ds_fin[r:P:32, :].bitcast(I32), ds_d[src:P:32, :].bitcast(I32))

        zb = tile([P, V, PACK], BF16, "zb")
        groups = ((0, 3), (3, 5), (5, 7), (7, 8))
        ln = [tile([P, hi - lo, 512], F32, "ln%d" % s) for s, (lo, hi) in enumerate(groups)]
        mx = [tile([P, hi - lo, 256], F32, "mx%d" % s) for s, (lo, hi) in enumerate(groups)]
        held = [None] * PACK

        def line_up(s):
            for i in range(*groups[s]):
                t, a = divmod(i, 2)
                nc.vector.tensor_copy(ln[s][:, i - groups[s][0], :], y[t][:].indirect(n1_t[:, 32 * a : 32 * a + 32]))

        def pool_pairs(s):
            pairs = ln[s][:].rearrange("p j (v two) -> p (j v) two", two=2)
            nc.vector.tensor_tensor(mx[s][:].rearrange("p j v -> p (j v)"), pairs[:, :, 0], pairs[:, :, 1], ALU.max)
            for i in range(*groups[s]):
                t, a = divmod(i, 2)
                nc.scalar.activation(
                    zb[:, 256 * a : 256 * (a + 1), t], mx[s][:, i - groups[s][0], :], COPY, scale=gs_t[:, t : t + 1]
                )

        def fetch_held(t, dst):
            held[t] = dst
            nc.vector.tensor_scalar(dst, page[t][:].indirect(n2_t[:]), 0.5, 0.0, ALU.mult, ALU.add)

        line_up(0)
        for s in range(1, 4):
            line_up(s)
            pool_pairs(s - 1)
        fetch_held(0, tile([P, V], F32, "held0", tag="y2")[:])
        pool_pairs(3)
        two = tile([P, 2, V], F32, "held12", tag="y3")
        fetch_held(1, two[:, 0, :])
        fetch_held(2, two[:, 1, :])

        zw = tile([P, V], U32, "zw")
        zs = tile([P, V], U8, "zs")
        nc.vector.quantize_mx(out=zw[:].bitcast(FP8X4), scales=zs[:], in_=zb[:].rearrange("p v t -> p (v t)"))
        hb = [ps.tile([P, V], F32, name="hb%d" % t, tag="bank%d" % t) for t in range(PACK)]
        for t in range(PACK):
            nc.tensor.matmul_mx(
                out=hb[t][:],
                lhsT=dw[:, P * t : P * (t + 1)].bitcast(FP8X4),
                lhsT_scale=ds_fin[:, P * t : P * (t + 1)],
                rhs=zw[:].bitcast(FP8X4),
                rhs_scale=zs[:],
                start=True,
                stop=True,
            )
        fetch_held(3, tile([P, V], F32, "held3", tag="mx3")[:])

        out_rows = out_0.rearrange("(p t) c -> p t c", t=PACK)
        spans = ((0, 512), (512, 768), (768, 1024))
        ob = [tile([P, hi - lo, PACK], BF16, "ob%d" % c) for c, (lo, hi) in enumerate(spans)]
        nw = [tile([P, V], F32, "nw%d" % t) for t in range(PACK)]

        def larger(t):
            nc.vector.scalar_tensor_tensor(nw[t][:], hb[t][:], 0.0625, held[t], ALU.mult, ALU.max)

        larger(0)
        for t in range(PACK):
            if t + 1 < PACK:
                larger(t + 1)
            nc.vector.tensor_copy(page[t][:].indirect(n2_t[:]), nw[t][:])
            nc.sync.dma_start(out_rows[:, t, :], page[t][:])
            if t == 2:
                nc.scalar.copy(ob[0][:, :, 2:4], page[t][:, 0:512].unsqueeze(2).to_broadcast([P, 512, 2]))
            elif t == 3:
                nc.vector.tensor_copy(ob[0][:, :, t], page[t][:, 0:512])
            else:
                nc.scalar.copy(ob[0][:, :, t], page[t][:, 0:512])
            for c in (1, 2):
                nc.scalar.copy(ob[c][:, :, t], page[t][:, spans[c][0] : spans[c][1]])

        osc = tile([P, U], U8, "osc")
        out_words = words_view(out_1)
        for c in (1, 0, 2):
            lo, hi = spans[c]
            ow = tile([P, hi - lo], I32, "ow%d" % c)
            nc.vector.quantize_mx(out=ow[:].bitcast(FP8X4), scales=osc[:, lo:hi], in_=ob[c][:].rearrange("p v t -> p (v t)"))
            nc.sync.dma_start(out_words[:, lo:hi], ow[:])
        for q in range(4):
            eng = nc.scalar if q % 2 else nc.sync
            eng.dma_start(out_2[0, 4 * q : 4 * q + 4, :].bitcast(I32), osc[32 * q : 32 * q + 4, :].bitcast(I32))
